import numpy as np
import ml_dtypes


def mxq(x, axis, fmt="e4m3"):
    dtype, down = {"e4m3": (ml_dtypes.float8_e4m3fn, 7), "e5m2": (ml_dtypes.float8_e5m2, 14)}[fmt]
    v = np.moveaxis(np.asarray(x, np.float32).astype(ml_dtypes.bfloat16).astype(np.float64), axis, -1)
    blocks = v.reshape(v.shape[:-1] + (-1, 32))
    amax = np.abs(blocks).max(-1, keepdims=True)
    byte = np.maximum(np.where(amax > 0, np.frexp(amax)[1] - 1 + 127, 0) - down, 1)
    scale = np.exp2(byte - 127.0)
    codes = (blocks / scale).astype(np.float32).astype(dtype).astype(np.float64)
    return np.moveaxis((codes * scale).reshape(v.shape), -1, axis)


WIDE = False


def mx_kscale(k):
    if not WIDE:
        return np.ones(k)
    levels = np.array([10, -10, 5, -5, 0])
    if k % 512:
        return np.exp2(np.random.permutation(np.resize(levels, k // 32))).repeat(32)
    a = np.empty((k // 512, 16))
    for p in range(k // 512):
        a[p, :8] = np.random.permutation(np.resize(levels, 8))
        for g in range(8):
            far = levels[np.abs(levels - a[p, g]) >= 10]
            a[p, g + 8] = far[np.random.randint(len(far))]
    return np.exp2(a.ravel()).repeat(32)


def f64(x):
    return np.asarray(x).astype(np.float64)


def striped(idx):
    return np.tile(idx.reshape(-1, 16).T, (8, 1)).astype(np.uint16)


def unstriped(offs):
    return offs[:16].T.reshape(-1).astype(np.int64)


def pack_weight(w):
    k, n = w.shape
    w = f64(np.asarray(w, np.float32).astype(ml_dtypes.bfloat16)).reshape(k // 32, 32, n)
    amax = np.abs(w).max(1)
    byte = np.clip(np.where(amax > 0, np.frexp(amax)[1] - 1 + 127 - 7, 1), 1, 254)
    scaled = (w * np.exp2(127.0 - byte)[:, None, :]).reshape(k, n).astype(np.float32)
    words = np.ascontiguousarray(scaled.reshape(k // 512, 128, 4, n).transpose(0, 1, 3, 2)).astype(ml_dtypes.float8_e4m3fn).view(np.uint8)
    return words, np.ascontiguousarray(byte.astype(np.uint8).reshape(k // 512, 16, n))


def unpack_weight(words, scales):
    g, p, n, _ = words.shape
    vals = np.ascontiguousarray(words).view(ml_dtypes.float8_e4m3fn).astype(np.float64) * np.repeat(np.exp2(scales.astype(np.float64) - 127.0), 8, axis=1)[..., None]
    return vals.transpose(0, 1, 3, 2).reshape(g * 512, n)


def relu(v):
    return np.maximum(v, 0.0)


K, T, S, V, H = 512, 1024, 512, 512, 512
P = 2 ** 7


def setup_inputs():
    n = np.random.standard_normal
    s = mx_kscale(K)[:, None]
    u = mx_kscale(H)
    packed_xT = pack_weight(n((K, T)) * s)
    return {
        "x_words": packed_xT[0],
        "x_scales": packed_xT[1],
        "w1": (n((K, H)) / np.sqrt(K) / s * u).astype(np.float32),
        "w2": (n((K, H)) / np.sqrt(K) / s / u / np.sqrt(H)).astype(np.float32),
        "head": (np.tile(0.5 * np.random.standard_normal(T), (P, 1))).astype(np.float32),
        "offs": striped(np.random.permutation(T)[:S]),
        "dst": striped(np.random.permutation(T)[:V]),
    }


def reference(x_words, x_scales, w1, w2, head, offs, dst):
    xq = unpack_weight(x_words, x_scales)[:, unstriped(offs)]
    p = relu(mxq(f64(w1), 0, "e4m3").T @ xq)
    x_dst = unpack_weight(x_words, x_scales)[:, unstriped(dst)]
    d = relu(mxq(f64(w2), 0, "e4m3").T @ x_dst)
    y = (mxq(p, 0, "e4m3").T @ mxq(d, 0, "e4m3")) + f64(head)[:1][:, unstriped(dst)]
    e = np.exp(y - y.max(axis=1, keepdims=True))
    return e / e.sum(axis=1, keepdims=True)

@@ -1,0 +1,191 @@
+from contextlib import ExitStack
+
+import concourse.mybir as mybir
+
+K, T, S, V, H = 512, 1024, 512, 512, 512
+FLOPS = 2 * K * H * S + 2 * K * H * V + 2 * H * S * V
+
+F32 = mybir.dt.float32
+BF16 = mybir.dt.bfloat16
+U32 = mybir.dt.uint32
+I32 = mybir.dt.int32
+U16 = mybir.dt.uint16
+U8 = mybir.dt.uint8
+FP8X4 = mybir.dt.float8_e4m3fn_x4
+ALU = mybir.AluOpType
+ACT = mybir.ActivationFunctionType
+AX = mybir.AxisListType
+
+P = 128
+PACK = 4
+TILES = 4
+
+
+def tile_picked_zarc_relu_p_kernel(tc, x_words, x_scales, w1, w2, head, offs, dst, out):
+    nc = tc.nc
+    with ExitStack() as ctx:
+        keep = ctx.enter_context(tc.tile_pool(name="keep", bufs=1))
+        psum = ctx.enter_context(tc.psum_pool(name="psum", bufs=8))
+
+        dst_list = keep.tile([P, V // 16], U16, name="dst_list")
+        offs_list = keep.tile([P, S // 16], U16, name="offs_list")
+        words = keep.tile([P, T], I32, name="words", align_bytes=64)
+        scales = keep.tile([P, T], U8, name="scales", align_bytes=64)
+        head_sb = keep.tile([P, T], F32, name="head_sb")
+
+        warm = keep.tile([P, 1], F32, name="warm")
+        warm_out = keep.tile([P, 1], F32, name="warm_out")
+        nc.vector.memset(warm[:], 0.0)
+        nc.scalar.activation(warm_out[:], warm[:], ACT.Exp)
+
+        w_raw = {}
+
+        def load_weight_half(w, name, u):
+            raw = keep.tile([P, PACK, H // 2], F32, name="%s_raw%d" % (name, u))
+            nc.sync.dma_start(raw[:], w.rearrange("(p j) c -> p j c", j=PACK)[:, :, u * H // 2 : (u + 1) * H // 2])
+            w_raw[name, u] = raw
+
+        nc.sync.dma_start(dst_list[:], dst)
+        scale_rows = x_scales[0].bitcast(I32)
+        for q in range(4):
+            queue = nc.scalar if q % 2 else nc.sync
+            queue.dma_start(
+                scales[32 * q : 32 * q + 32, :].bitcast(I32),
+                scale_rows[4 * q : 4 * q + 4, :].unsqueeze(0).to_broadcast([8, 4, T // 4]),
+            )
+        nc.sync.dma_start(offs_list[:], offs)
+        load_weight_half(w2, "w2", 0)
+        nc.sync.dma_start(words[:], x_words[0].rearrange("p c r -> p (c r)").bitcast(I32))
+        load_weight_half(w2, "w2", 1)
+        load_weight_half(w1, "w1", 0)
+        load_weight_half(w1, "w1", 1)
+        nc.sync.dma_start(head_sb[:], head)
+
+        def gather_scales(index_list, name):
+            planes = keep.tile([P, S], U8, name=name + "_scales", align_bytes=64)
+            nc.vector.tensor_copy(planes[:], scales[:].indirect(index_list[:]))
+            return planes
+
+        def gather_words(index_list, name, tag=None):
+            codes = keep.tile([P, S], U32, name=name + "_codes", tag=tag or name + "_codes", align_bytes=64)
+            nc.vector.tensor_copy(codes[:], words[:].bitcast(U32).indirect(index_list[:]))
+            return codes
+
+        def cast_scalar(woven, raw, u, t0, tn):
+            nc.scalar.copy(
+                woven.rearrange("p (t a i j) -> p a t j i", t=tn, i=4, j=4)[:, 16 * u : 16 * u + 16],
+                raw[:].rearrange("p j (a t i) -> p a t j i", t=4, i=4)[:, :, t0 : t0 + tn],
+            )
+
+        def cast_gpsimd(woven, raw, u, t0, tn):
+            nc.gpsimd.tensor_scalar(
+                woven.rearrange("p (t a i j) -> p a t i j", t=tn, i=4, j=4)[:, 16 * u : 16 * u + 16],
+                raw[:].rearrange("p j (a t i) -> p a t i j", t=4, i=4)[:, :, t0 : t0 + tn],
+                1.0, 0.0, ALU.mult, ALU.add,
+            )
+
+        def quantize(pieces, name):
+            width = sum(piece.shape[1] for piece in pieces) // PACK
+            codes = keep.tile([P, width], U32, name=name + "_codes", align_bytes=64)
+            planes = keep.tile([P, width], U8, name=name + "_scales", align_bytes=64)
+            first = 0
+            for piece in pieces:
+                cols = slice(first, first + piece.shape[1] // PACK)
+                nc.vector.quantize_mx(out=codes[:, cols].bitcast(FP8X4), scales=planes[:, cols], in_=piece)
+                first = cols.stop
+            return codes, planes
+
+        def tower(weight, picked, n, hidden):
+            bank = psum.tile([P, PACK, P], F32, name="bank")
+            cols = slice(n * P, (n + 1) * P)
+            for t in range(PACK):
+                rows = slice(t * P, (t + 1) * P)
+                nc.tensor.matmul_mx(
+                    out=bank[:, t, :],
+                    lhsT=weight[0][:, rows].bitcast(FP8X4),
+                    lhsT_scale=weight[1][:, rows],
+                    rhs=picked[0][:, cols].bitcast(FP8X4),
+                    rhs_scale=picked[1][:, cols],
+                    start=True,
+                    stop=True,
+                )
+            nc.scalar.activation(hidden.rearrange("p (n t) -> p n t", t=PACK), bank[:].rearrange("p t n -> p n t"), ACT.Relu)
+
+        dst_scales = gather_scales(dst_list, "x_dst")
+        offs_scales = gather_scales(offs_list, "x_offs")
+        x_dst = (gather_words(dst_list, "x_dst"), dst_scales)
+
+        w2_low = keep.tile([P, 2 * P * PACK], BF16, name="w2_low", align_bytes=64)
+        w2_high = keep.tile([P, 2 * P * PACK], BF16, name="w2_high", align_bytes=64)
+        cast_scalar(w2_low[:], w_raw["w2", 0], 0, 0, 2)
+        cast_scalar(w2_high[:], w_raw["w2", 0], 0, 2, 2)
+        cast_scalar(w2_low[:], w_raw["w2", 1], 1, 0, 2)
+        cast_gpsimd(w2_high[:], w_raw["w2", 1], 1, 2, 2)
+        w2_mx = quantize([w2_low[:], w2_high[:]], "w2")
+        x_offs = (gather_words(offs_list, "x_offs", tag="w2_high"), offs_scales)
+
+        w1_bf = keep.tile([P, H * PACK], BF16, name="w1_bf", align_bytes=64)
+        cast_gpsimd(w1_bf[:], w_raw["w1", 0], 0, 0, 4)
+        cast_gpsimd(w1_bf[:], w_raw["w1", 1], 1, 0, 4)
+
+        d_bf = keep.tile([P, V * PACK], BF16, name="d_bf", align_bytes=64)
+        for n in range(TILES):
+            tower(w2_mx, x_dst, n, d_bf[:, n * P * PACK : (n + 1) * P * PACK])
+        head_dst = keep.tile([P, V], F32, name="head_dst")
+        nc.vector.tensor_copy(head_dst[:], head_sb[:].indirect(dst_list[:]))
+        w1_mx = quantize([w1_bf[:]], "w1")
+        d_mx = quantize([d_bf[:]], "d")
+
+        minus_y, minus_max, e, total = {}, {}, {}, {}
+
+        def scores_of(n):
+            p_bf = keep.tile([P, P * PACK], BF16, name="p_bf%d" % n, align_bytes=64)
+            tower(w1_mx, x_offs, n, p_bf[:])
+            return quantize([p_bf[:]], "p%d" % n)
+
+        def add_head(n, p_mx):
+            bank = psum.tile([P, PACK, P], F32, name="bank")
+            scores = bank[:].rearrange("p t n -> p (t n)")
+            nc.tensor.matmul_mx(
+                out=scores,
+                lhsT=p_mx[0][:].bitcast(FP8X4),
+                lhsT_scale=p_mx[1][:],
+                rhs=d_mx[0][:].bitcast(FP8X4),
+                rhs_scale=d_mx[1][:],
+                start=True,
+                stop=True,
+            )
+            tag = "total%d" % (n - 3) if n >= 3 else "minus_y%d" % n
+            minus_y[n] = keep.tile([P, V], F32, name="minus_y%d" % n, tag=tag)
+            nc.vector.scalar_tensor_tensor(minus_y[n][:], scores, -1.0, head_dst[:], ALU.mult, ALU.subtract)
+
+        def exponentiate(n):
+            minus_max[n] = keep.tile([P, 1], F32, name="minus_max%d" % n)
+            nc.vector.tensor_reduce(minus_max[n][:], minus_y[n][:], AX.X, ALU.min)
+            e[n] = keep.tile([P, V], F32, name="e%d" % n)
+            total[n] = keep.tile([P, 1], F32, name="total%d" % n)
+            nc.scalar.activation(e[n][:], minus_y[n][:], ACT.Exp, bias=minus_max[n][:], scale=-1.0, accum_out=total[n][:])
+
+        def normalise(n):
+            inverse = keep.tile([P, 1], F32, name="inverse%d" % n)
+            nc.vector.reciprocal(inverse[:], total[n][:])
+            result = keep.tile([P, V], F32, name="result%d" % n)
+            if n < TILES - 1:
+                nc.gpsimd.tensor_scalar(result[:], e[n][:], inverse[:], 0.0, ALU.mult, ALU.add)
+            else:
+                nc.vector.tensor_scalar(result[:], e[n][:], inverse[:], None, ALU.mult)
+            nc.sync.dma_start(out[n * P : (n + 1) * P, :], result[:])
+
+        p_mx = [scores_of(n) for n in range(TILES)]
+        add_head(0, p_mx[0])
+        add_head(1, p_mx[1])
+        exponentiate(0)
+        add_head(2, p_mx[2])
+        exponentiate(1)
+        normalise(0)
+        add_head(3, p_mx[3])
+        exponentiate(2)
+        normalise(1)
+        exponentiate(3)
+        normalise(2)
+        normalise(3)

@@ -55,8 +55,8 @@ def tile_picked_zarc_relu_p_kernel(tc, x_words, x_scales, w1, w2, head, offs, ds
             )
         nc.sync.dma_start(offs_list[:], offs)
         load_weight_half(w2, "w2", 0)
-        nc.sync.dma_start(words[:], x_words[0].rearrange("p c r -> p (c r)").bitcast(I32))
         load_weight_half(w2, "w2", 1)
+        nc.sync.dma_start(words[:], x_words[0].rearrange("p c r -> p (c r)").bitcast(I32))
         load_weight_half(w1, "w1", 0)
         load_weight_half(w1, "w1", 1)
         nc.sync.dma_start(head_sb[:], head)
@@ -66,9 +66,12 @@ def tile_picked_zarc_relu_p_kernel(tc, x_words, x_scales, w1, w2, head, offs, ds
             nc.vector.tensor_copy(planes[:], scales[:].indirect(index_list[:]))
             return planes
 
-        def gather_words(index_list, name, tag=None):
-            codes = keep.tile([P, S], U32, name=name + "_codes", tag=tag or name + "_codes", align_bytes=64)
-            nc.vector.tensor_copy(codes[:], words[:].bitcast(U32).indirect(index_list[:]))
+        def gather_words(index_list, name, pieces):
+            codes = keep.tile([P, S], U32, name=name + "_codes", align_bytes=64)
+            width = S // pieces
+            for u in range(pieces):
+                entries = index_list[:, u * width // 16 : (u + 1) * width // 16]
+                nc.vector.tensor_copy(codes[:, u * width : (u + 1) * width], words[:].bitcast(U32).indirect(entries))
             return codes
 
         def cast_scalar(woven, raw, u, t0, tn):
@@ -77,11 +80,10 @@ def tile_picked_zarc_relu_p_kernel(tc, x_words, x_scales, w1, w2, head, offs, ds
                 raw[:].rearrange("p j (a t i) -> p a t j i", t=4, i=4)[:, :, t0 : t0 + tn],
             )
 
-        def cast_gpsimd(woven, raw, u, t0, tn):
-            nc.gpsimd.tensor_scalar(
-                woven.rearrange("p (t a i j) -> p a t i j", t=tn, i=4, j=4)[:, 16 * u : 16 * u + 16],
-                raw[:].rearrange("p j (a t i) -> p a t i j", t=4, i=4)[:, :, t0 : t0 + tn],
-                1.0, 0.0, ALU.mult, ALU.add,
+        def cast_vector(woven, raw, u, t0, tn):
+            nc.vector.tensor_copy(
+                woven.rearrange("p (t a i j) -> p a t j i", t=tn, i=4, j=4)[:, 16 * u : 16 * u + 16],
+                raw[:].rearrange("p j (a t i) -> p a t j i", t=4, i=4)[:, :, t0 : t0 + tn],
             )
 
         def quantize(pieces, name):
@@ -95,7 +97,7 @@ def tile_picked_zarc_relu_p_kernel(tc, x_words, x_scales, w1, w2, head, offs, ds
                 first = cols.stop
             return codes, planes
 
-        def tower(weight, picked, n, hidden):
+        def tower(weight, picked, n, hidden, on_vector=False):
             bank = psum.tile([P, PACK, P], F32, name="bank")
             cols = slice(n * P, (n + 1) * P)
             for t in range(PACK):
@@ -109,31 +111,37 @@ def tile_picked_zarc_relu_p_kernel(tc, x_words, x_scales, w1, w2, head, offs, ds
                     start=True,
                     stop=True,
                 )
-            nc.scalar.activation(hidden.rearrange("p (n t) -> p n t", t=PACK), bank[:].rearrange("p t n -> p n t"), ACT.Relu)
+            woven = hidden.rearrange("p (n t) -> p n t", t=PACK)
+            sums = bank[:].rearrange("p t n -> p n t")
+            if on_vector:
+                nc.vector.tensor_scalar(woven, sums, 0.0, None, ALU.max)
+            else:
+                nc.scalar.activation(woven, sums, ACT.Relu)
 
         dst_scales = gather_scales(dst_list, "x_dst")
         offs_scales = gather_scales(offs_list, "x_offs")
-        x_dst = (gather_words(dst_list, "x_dst"), dst_scales)
 
         w2_low = keep.tile([P, 2 * P * PACK], BF16, name="w2_low", align_bytes=64)
         w2_high = keep.tile([P, 2 * P * PACK], BF16, name="w2_high", align_bytes=64)
         cast_scalar(w2_low[:], w_raw["w2", 0], 0, 0, 2)
         cast_scalar(w2_high[:], w_raw["w2", 0], 0, 2, 2)
         cast_scalar(w2_low[:], w_raw["w2", 1], 1, 0, 2)
-        cast_gpsimd(w2_high[:], w_raw["w2", 1], 1, 2, 2)
+        cast_vector(w2_high[:], w_raw["w2", 1], 1, 2, 2)
         w2_mx = quantize([w2_low[:], w2_high[:]], "w2")
-        x_offs = (gather_words(offs_list, "x_offs", tag="w2_high"), offs_scales)
+        x_dst = (gather_words(dst_list, "x_dst", 2), dst_scales)
+        x_offs = (gather_words(offs_list, "x_offs", 1), offs_scales)
 
         w1_bf = keep.tile([P, H * PACK], BF16, name="w1_bf", align_bytes=64)
-        cast_gpsimd(w1_bf[:], w_raw["w1", 0], 0, 0, 4)
-        cast_gpsimd(w1_bf[:], w_raw["w1", 1], 1, 0, 4)
+        cast_scalar(w1_bf[:], w_raw["w1", 0], 0, 0, 4)
+        cast_scalar(w1_bf[:, : 2 * P * PACK], w_raw["w1", 1], 1, 0, 2)
+        cast_vector(w1_bf[:, 2 * P * PACK :], w_raw["w1", 1], 1, 2, 2)
 
         d_bf = keep.tile([P, V * PACK], BF16, name="d_bf", align_bytes=64)
         for n in range(TILES):
             tower(w2_mx, x_dst, n, d_bf[:, n * P * PACK : (n + 1) * P * PACK])
+        w1_mx = quantize([w1_bf[:, : 2 * P * PACK], w1_bf[:, 2 * P * PACK :]], "w1")
         head_dst = keep.tile([P, V], F32, name="head_dst")
         nc.vector.tensor_copy(head_dst[:], head_sb[:].indirect(dst_list[:]))
-        w1_mx = quantize([w1_bf[:]], "w1")
         d_mx = quantize([d_bf[:]], "d")
 
         minus_y, minus_max, e, total = {}, {}, {}, {}
@@ -172,9 +180,12 @@ def tile_picked_zarc_relu_p_kernel(tc, x_words, x_scales, w1, w2, head, offs, ds
             result = keep.tile([P, V], F32, name="result%d" % n)
             if n < TILES - 1:
                 nc.gpsimd.tensor_scalar(result[:], e[n][:], inverse[:], 0.0, ALU.mult, ALU.add)
+                nc.sync.dma_start(out[n * P : (n + 1) * P, :], result[:])
             else:
-                nc.vector.tensor_scalar(result[:], e[n][:], inverse[:], None, ALU.mult)
-            nc.sync.dma_start(out[n * P : (n + 1) * P, :], result[:])
+                for u, queue in enumerate((nc.sync, nc.scalar)):
+                    cols = slice(u * V // 2, (u + 1) * V // 2)
+                    nc.vector.tensor_scalar(result[:, cols], e[n][:, cols], inverse[:], None, ALU.mult)
+                    queue.dma_start(out[n * P : (n + 1) * P, cols], result[:, cols])
 
         p_mx = [scores_of(n) for n in range(TILES)]
         add_head(0, p_mx[0])

@@ -1,6 +1,7 @@
 from contextlib import ExitStack
 
 import concourse.mybir as mybir
+from concourse.masks import make_identity
 
 K, T, S, V, H = 512, 1024, 512, 512, 512
 FLOPS = 2 * K * H * S + 2 * K * H * V + 2 * H * S * V
@@ -38,10 +39,13 @@ def tile_picked_zarc_relu_p_kernel(tc, x_words, x_scales, w1, w2, head, offs, ds
         nc.vector.memset(warm[:], 0.0)
         nc.scalar.activation(warm_out[:], warm[:], ACT.Exp)
 
+        identity = keep.tile([P, P], F32, name="identity")
+        make_identity(nc, identity[:])
+
         w_raw = {}
 
         def load_weight_half(w, name, u):
-            raw = keep.tile([P, PACK, H // 2], F32, name="%s_raw%d" % (name, u))
+            raw = keep.tile([P, PACK, H // 2], F32, name="%s_raw%d" % (name, u), align_bytes=64)
             nc.sync.dma_start(raw[:], w.rearrange("(p j) c -> p j c", j=PACK)[:, :, u * H // 2 : (u + 1) * H // 2])
             w_raw[name, u] = raw
 
@@ -133,70 +137,107 @@ def tile_picked_zarc_relu_p_kernel(tc, x_words, x_scales, w1, w2, head, offs, ds
 
         w1_bf = keep.tile([P, H * PACK], BF16, name="w1_bf", align_bytes=64)
         cast_scalar(w1_bf[:], w_raw["w1", 0], 0, 0, 4)
-        cast_scalar(w1_bf[:, : 2 * P * PACK], w_raw["w1", 1], 1, 0, 2)
-        cast_vector(w1_bf[:, 2 * P * PACK :], w_raw["w1", 1], 1, 2, 2)
+        cast_scalar(w1_bf[:], w_raw["w1", 1], 1, 0, 4)
 
-        d_bf = keep.tile([P, V * PACK], BF16, name="d_bf", align_bytes=64)
-        for n in range(TILES):
-            tower(w2_mx, x_dst, n, d_bf[:, n * P * PACK : (n + 1) * P * PACK])
-        w1_mx = quantize([w1_bf[:, : 2 * P * PACK], w1_bf[:, 2 * P * PACK :]], "w1")
-        head_dst = keep.tile([P, V], F32, name="head_dst")
+        d_first = keep.tile([P, P * PACK], BF16, name="d_first", align_bytes=64)
+        d_rest = keep.tile([P, 3 * P * PACK], BF16, name="d_rest", tag="w1_raw1", align_bytes=64)
+        tower(w2_mx, x_dst, 0, d_first[:], on_vector=True)
+        for n in range(1, TILES):
+            tower(w2_mx, x_dst, n, d_rest[:, (n - 1) * P * PACK : n * P * PACK])
+        w1_mx = quantize([w1_bf[:]], "w1")
+        head_dst = keep.tile([P, V], F32, name="head_dst", tag="w1_bf", align_bytes=64)
         nc.vector.tensor_copy(head_dst[:], head_sb[:].indirect(dst_list[:]))
-        d_mx = quantize([d_bf[:]], "d")
+        d_mx = quantize([d_first[:], d_rest[:, : P * PACK], d_rest[:, P * PACK :]], "d")
 
-        minus_y, minus_max, e, total = {}, {}, {}, {}
+        minus_y, e, total = {}, {}, {}
 
-        def scores_of(n):
+        def dependents(n):
             p_bf = keep.tile([P, P * PACK], BF16, name="p_bf%d" % n, align_bytes=64)
             tower(w1_mx, x_offs, n, p_bf[:])
             return quantize([p_bf[:]], "p%d" % n)
 
-        def add_head(n, p_mx):
+        def scores_by_rows(n):
             bank = psum.tile([P, PACK, P], F32, name="bank")
             scores = bank[:].rearrange("p t n -> p (t n)")
             nc.tensor.matmul_mx(
                 out=scores,
-                lhsT=p_mx[0][:].bitcast(FP8X4),
-                lhsT_scale=p_mx[1][:],
+                lhsT=p_mx[n][0][:].bitcast(FP8X4),
+                lhsT_scale=p_mx[n][1][:],
                 rhs=d_mx[0][:].bitcast(FP8X4),
                 rhs_scale=d_mx[1][:],
                 start=True,
                 stop=True,
             )
-            tag = "total%d" % (n - 3) if n >= 3 else "minus_y%d" % n
-            minus_y[n] = keep.tile([P, V], F32, name="minus_y%d" % n, tag=tag)
-            nc.vector.scalar_tensor_tensor(minus_y[n][:], scores, -1.0, head_dst[:], ALU.mult, ALU.subtract)
+            summed = keep.tile([P, V], F32, name="minus_y%d" % n)
+            nc.vector.scalar_tensor_tensor(summed[:], scores, -1.0, head_dst[:], ALU.mult, ALU.subtract)
+            minus_y[n] = summed[:]
+
+        def scores_by_columns(n):
+            bank = psum.tile([P, PACK, P], F32, name="bank")
+            turned = keep.tile([P, TILES, P], F32, name="turned%d" % n)
+            for b in range(TILES):
+                cols = slice(b * P, (b + 1) * P)
+                nc.tensor.matmul_mx(
+                    out=bank[:, b, :],
+                    lhsT=d_mx[0][:, cols].bitcast(FP8X4),
+                    lhsT_scale=d_mx[1][:, cols],
+                    rhs=p_mx[n][0][:].bitcast(FP8X4),
+                    rhs_scale=p_mx[n][1][:],
+                    start=True,
+                    stop=True,
+                )
+            for b in range(TILES):
+                nc.scalar.activation(turned[:, b, :], bank[:, b, :], ACT.Identity, bias=minus_head[:, b : b + 1], scale=-1.0)
+            return turned
+
+        def turn_back(n, turned):
+            bank = psum.tile([P, PACK, P], F32, name="bank")
+            for b in range(TILES):
+                nc.tensor.transpose(bank[:, b, :], turned[:, b, :], identity[:])
+            minus_y[n] = bank[:].rearrange("p t n -> p (t n)")
 
         def exponentiate(n):
-            minus_max[n] = keep.tile([P, 1], F32, name="minus_max%d" % n)
-            nc.vector.tensor_reduce(minus_max[n][:], minus_y[n][:], AX.X, ALU.min)
+            minus_max = keep.tile([P, 1], F32, name="minus_max%d" % n, tag="total0" if n == 3 else "minus_max%d" % n)
+            nc.vector.tensor_reduce(minus_max[:], minus_y[n], AX.X, ALU.min)
             e[n] = keep.tile([P, V], F32, name="e%d" % n)
             total[n] = keep.tile([P, 1], F32, name="total%d" % n)
-            nc.scalar.activation(e[n][:], minus_y[n][:], ACT.Exp, bias=minus_max[n][:], scale=-1.0, accum_out=total[n][:])
+            nc.scalar.activation(e[n][:], minus_y[n], ACT.Exp, bias=minus_max[:], scale=-1.0, accum_out=total[n][:])
 
-        def normalise(n):
+        def normalise(n, last=False):
             inverse = keep.tile([P, 1], F32, name="inverse%d" % n)
             nc.vector.reciprocal(inverse[:], total[n][:])
             result = keep.tile([P, V], F32, name="result%d" % n)
-            if n < TILES - 1:
-                nc.gpsimd.tensor_scalar(result[:], e[n][:], inverse[:], 0.0, ALU.mult, ALU.add)
-                nc.sync.dma_start(out[n * P : (n + 1) * P, :], result[:])
-            else:
+            if last:
                 for u, queue in enumerate((nc.sync, nc.scalar)):
                     cols = slice(u * V // 2, (u + 1) * V // 2)
                     nc.vector.tensor_scalar(result[:, cols], e[n][:, cols], inverse[:], None, ALU.mult)
                     queue.dma_start(out[n * P : (n + 1) * P, cols], result[:, cols])
+            else:
+                if n > 0:
+                    nc.vector.tensor_scalar(result[:], e[n][:], inverse[:], None, ALU.mult)
+                else:
+                    nc.gpsimd.tensor_scalar(result[:], e[n][:], inverse[:], 0.0, ALU.mult, ALU.add)
+                nc.sync.dma_start(out[n * P : (n + 1) * P, :], result[:])
 
-        p_mx = [scores_of(n) for n in range(TILES)]
-        add_head(0, p_mx[0])
-        add_head(1, p_mx[1])
+        p_mx = [dependents(n) for n in range(TILES)]
+
+        head_bank = psum.tile([P, PACK, P], F32, name="bank")
+        for b in range(TILES):
+            nc.tensor.transpose(head_bank[:, b, :], head_dst[:, b * P : (b + 1) * P], identity[:])
+        minus_head = keep.tile([P, TILES], F32, name="minus_head")
+        nc.scalar.activation(minus_head[:], head_bank[:, :, 0], ACT.Copy, scale=-1.0)
+
+        scores_by_rows(0)
+        turned1 = scores_by_columns(1)
+        scores_by_rows(2)
+        turned3 = scores_by_columns(3)
         exponentiate(0)
-        add_head(2, p_mx[2])
+        turn_back(1, turned1)
+        exponentiate(2)
+        turn_back(3, turned3)
         exponentiate(1)
         normalise(0)
-        add_head(3, p_mx[3])
-        exponentiate(2)
-        normalise(1)
         exponentiate(3)
         normalise(2)
-        normalise(3)
+        normalise(1)
+        normalise(3, last=True)

@@ -20,101 +20,100 @@ AX = mybir.AxisListType
 P = 128
 PACK = 4
 TILES = 4
+BANKS = 8
+QUADRANT = 32
+LIST_ROWS = 16
+RUN = 4
+HALF_GROUPS = H // 2 // (PACK * RUN)
+TILE_VALUES = P * PACK
+MX_ALIGN = 64
+LAST_VECTOR_COLUMNS = 320
 
 
 def tile_picked_zarc_relu_p_kernel(tc, x_words, x_scales, w1, w2, head, offs, dst, out):
     nc = tc.nc
     with ExitStack() as ctx:
         keep = ctx.enter_context(tc.tile_pool(name="keep", bufs=1))
-        psum = ctx.enter_context(tc.psum_pool(name="psum", bufs=8))
+        psum = ctx.enter_context(tc.psum_pool(name="psum", bufs=BANKS))
 
-        dst_list = keep.tile([P, V // 16], U16, name="dst_list")
-        offs_list = keep.tile([P, S // 16], U16, name="offs_list")
-        words = keep.tile([P, T], I32, name="words", align_bytes=64)
-        scales = keep.tile([P, T], U8, name="scales", align_bytes=64)
+        dst_list = keep.tile([P, V // LIST_ROWS], U16, name="dst_list")
+        offs_list = keep.tile([P, S // LIST_ROWS], U16, name="offs_list")
+        words = keep.tile([P, T], I32, name="words", align_bytes=MX_ALIGN)
+        scales = keep.tile([P, T], U8, name="scales", align_bytes=MX_ALIGN)
         head_sb = keep.tile([P, T], F32, name="head_sb")
-
-        warm = keep.tile([P, 1], F32, name="warm")
-        warm_out = keep.tile([P, 1], F32, name="warm_out")
-        nc.vector.memset(warm[:], 0.0)
-        nc.scalar.activation(warm_out[:], warm[:], ACT.Exp)
 
         identity = keep.tile([P, P], F32, name="identity")
         make_identity(nc, identity[:])
 
-        w_raw = {}
-
-        def load_weight_half(w, name, u):
-            raw = keep.tile([P, PACK, H // 2], F32, name="%s_raw%d" % (name, u), align_bytes=64)
-            nc.sync.dma_start(raw[:], w.rearrange("(p j) c -> p j c", j=PACK)[:, :, u * H // 2 : (u + 1) * H // 2])
-            w_raw[name, u] = raw
+        def load_weight_half(w, name, half):
+            raw = keep.tile([P, PACK, H // 2], F32, name="%s_raw%d" % (name, half), align_bytes=MX_ALIGN)
+            cols = slice(half * H // 2, (half + 1) * H // 2)
+            nc.sync.dma_start(raw[:], w.rearrange("(p j) c -> p j c", j=PACK)[:, :, cols])
+            return raw
 
         nc.sync.dma_start(dst_list[:], dst)
         scale_rows = x_scales[0].bitcast(I32)
-        for q in range(4):
+        for q in range(P // QUADRANT):
             queue = nc.scalar if q % 2 else nc.sync
             queue.dma_start(
-                scales[32 * q : 32 * q + 32, :].bitcast(I32),
-                scale_rows[4 * q : 4 * q + 4, :].unsqueeze(0).to_broadcast([8, 4, T // 4]),
+                scales[QUADRANT * q : QUADRANT * (q + 1), :].bitcast(I32),
+                scale_rows[4 * q : 4 * q + 4, :].unsqueeze(0).to_broadcast([QUADRANT // 4, 4, T // 4]),
             )
         nc.sync.dma_start(offs_list[:], offs)
-        load_weight_half(w2, "w2", 0)
-        load_weight_half(w2, "w2", 1)
+        w2_raw = [load_weight_half(w2, "w2", half) for half in range(2)]
         nc.sync.dma_start(words[:], x_words[0].rearrange("p c r -> p (c r)").bitcast(I32))
-        load_weight_half(w1, "w1", 0)
-        load_weight_half(w1, "w1", 1)
+        w1_raw = [load_weight_half(w1, "w1", half) for half in range(2)]
         nc.sync.dma_start(head_sb[:], head)
 
         def gather_scales(index_list, name):
-            planes = keep.tile([P, S], U8, name=name + "_scales", align_bytes=64)
-            nc.vector.tensor_copy(planes[:], scales[:].indirect(index_list[:]))
-            return planes
+            picked = keep.tile([P, S], U8, name=name + "_scales", align_bytes=MX_ALIGN)
+            nc.vector.tensor_copy(picked[:], scales[:].indirect(index_list[:]))
+            return picked
 
-        def gather_words(index_list, name, pieces):
-            codes = keep.tile([P, S], U32, name=name + "_codes", align_bytes=64)
+        def gather_words(index_list, name, pieces, tag):
+            picked = keep.tile([P, S], U32, name=name + "_codes", tag=tag, align_bytes=MX_ALIGN)
             width = S // pieces
             for u in range(pieces):
-                entries = index_list[:, u * width // 16 : (u + 1) * width // 16]
-                nc.vector.tensor_copy(codes[:, u * width : (u + 1) * width], words[:].bitcast(U32).indirect(entries))
-            return codes
+                entries = index_list[:, u * width // LIST_ROWS : (u + 1) * width // LIST_ROWS]
+                nc.vector.tensor_copy(picked[:, u * width : (u + 1) * width], words[:].bitcast(U32).indirect(entries))
+            return picked
 
-        def cast_scalar(woven, raw, u, t0, tn):
-            nc.scalar.copy(
-                woven.rearrange("p (t a i j) -> p a t j i", t=tn, i=4, j=4)[:, 16 * u : 16 * u + 16],
-                raw[:].rearrange("p j (a t i) -> p a t j i", t=4, i=4)[:, :, t0 : t0 + tn],
-            )
-
-        def cast_vector(woven, raw, u, t0, tn):
-            nc.vector.tensor_copy(
-                woven.rearrange("p (t a i j) -> p a t j i", t=tn, i=4, j=4)[:, 16 * u : 16 * u + 16],
-                raw[:].rearrange("p j (a t i) -> p a t j i", t=4, i=4)[:, :, t0 : t0 + tn],
+        def round_weight(copy, woven, raw, half, first_slot, slots):
+            groups = slice(HALF_GROUPS * half, HALF_GROUPS * (half + 1))
+            copy(
+                woven.rearrange("p (t a r j) -> p a t j r", t=slots, r=RUN, j=PACK)[:, groups],
+                raw[:].rearrange("p j (a t r) -> p a t j r", t=PACK, r=RUN)[:, :, first_slot : first_slot + slots],
             )
 
         def quantize(pieces, name):
             width = sum(piece.shape[1] for piece in pieces) // PACK
-            codes = keep.tile([P, width], U32, name=name + "_codes", align_bytes=64)
-            planes = keep.tile([P, width], U8, name=name + "_scales", align_bytes=64)
+            codes = keep.tile([P, width], U32, name=name + "_codes", align_bytes=MX_ALIGN)
+            scale_bytes = keep.tile([P, width], U8, name=name + "_scales", align_bytes=MX_ALIGN)
             first = 0
             for piece in pieces:
                 cols = slice(first, first + piece.shape[1] // PACK)
-                nc.vector.quantize_mx(out=codes[:, cols].bitcast(FP8X4), scales=planes[:, cols], in_=piece)
+                nc.vector.quantize_mx(out=codes[:, cols].bitcast(FP8X4), scales=scale_bytes[:, cols], in_=piece)
                 first = cols.stop
-            return codes, planes
+            return codes, scale_bytes
+
+        def multiply(result, stationary, stationary_cols, moving, moving_cols):
+            nc.tensor.matmul_mx(
+                out=result,
+                lhsT=stationary[0][:, stationary_cols].bitcast(FP8X4),
+                lhsT_scale=stationary[1][:, stationary_cols],
+                rhs=moving[0][:, moving_cols].bitcast(FP8X4),
+                rhs_scale=moving[1][:, moving_cols],
+                start=True,
+                stop=True,
+            )
+
+        def block(n):
+            return slice(n * P, (n + 1) * P)
 
         def tower(weight, picked, n, hidden, on_vector=False):
             bank = psum.tile([P, PACK, P], F32, name="bank")
-            cols = slice(n * P, (n + 1) * P)
             for t in range(PACK):
-                rows = slice(t * P, (t + 1) * P)
-                nc.tensor.matmul_mx(
-                    out=bank[:, t, :],
-                    lhsT=weight[0][:, rows].bitcast(FP8X4),
-                    lhsT_scale=weight[1][:, rows],
-                    rhs=picked[0][:, cols].bitcast(FP8X4),
-                    rhs_scale=picked[1][:, cols],
-                    start=True,
-                    stop=True,
-                )
+                multiply(bank[:, t, :], weight, block(t), picked, block(n))
             woven = hidden.rearrange("p (n t) -> p n t", t=PACK)
             sums = bank[:].rearrange("p t n -> p n t")
             if on_vector:
@@ -125,119 +124,103 @@ def tile_picked_zarc_relu_p_kernel(tc, x_words, x_scales, w1, w2, head, offs, ds
         dst_scales = gather_scales(dst_list, "x_dst")
         offs_scales = gather_scales(offs_list, "x_offs")
 
-        w2_low = keep.tile([P, 2 * P * PACK], BF16, name="w2_low", align_bytes=64)
-        w2_high = keep.tile([P, 2 * P * PACK], BF16, name="w2_high", align_bytes=64)
-        cast_scalar(w2_low[:], w_raw["w2", 0], 0, 0, 2)
-        cast_scalar(w2_high[:], w_raw["w2", 0], 0, 2, 2)
-        cast_scalar(w2_low[:], w_raw["w2", 1], 1, 0, 2)
-        cast_vector(w2_high[:], w_raw["w2", 1], 1, 2, 2)
+        w2_low = keep.tile([P, 2 * TILE_VALUES], BF16, name="w2_low", align_bytes=MX_ALIGN)
+        w2_high = keep.tile([P, 2 * TILE_VALUES], BF16, name="w2_high", align_bytes=MX_ALIGN)
+        round_weight(nc.scalar.copy, w2_low[:], w2_raw[0], 0, 0, 2)
+        round_weight(nc.scalar.copy, w2_high[:], w2_raw[0], 0, 2, 2)
+        round_weight(nc.scalar.copy, w2_low[:], w2_raw[1], 1, 0, 2)
+        round_weight(nc.vector.tensor_copy, w2_high[:], w2_raw[1], 1, 2, 2)
         w2_mx = quantize([w2_low[:], w2_high[:]], "w2")
-        x_dst = (gather_words(dst_list, "x_dst", 2), dst_scales)
-        x_offs = (gather_words(offs_list, "x_offs", 1), offs_scales)
+        x_dst = (gather_words(dst_list, "x_dst", 2, "w2_high"), dst_scales)
+        x_offs = (gather_words(offs_list, "x_offs", 1, "w2_low"), offs_scales)
 
-        w1_bf = keep.tile([P, H * PACK], BF16, name="w1_bf", align_bytes=64)
-        cast_scalar(w1_bf[:], w_raw["w1", 0], 0, 0, 4)
-        cast_scalar(w1_bf[:], w_raw["w1", 1], 1, 0, 4)
+        w1_bf = keep.tile([P, H * PACK], BF16, name="w1_bf", align_bytes=MX_ALIGN)
+        for half in range(2):
+            round_weight(nc.scalar.copy, w1_bf[:], w1_raw[half], half, 0, PACK)
 
-        d_first = keep.tile([P, P * PACK], BF16, name="d_first", align_bytes=64)
-        d_rest = keep.tile([P, 3 * P * PACK], BF16, name="d_rest", tag="w1_raw1", align_bytes=64)
+        d_first = keep.tile([P, TILE_VALUES], BF16, name="d_first", align_bytes=MX_ALIGN)
+        d_rest = keep.tile([P, (TILES - 1) * TILE_VALUES], BF16, name="d_rest", tag="w1_raw1", align_bytes=MX_ALIGN)
         tower(w2_mx, x_dst, 0, d_first[:], on_vector=True)
         for n in range(1, TILES):
-            tower(w2_mx, x_dst, n, d_rest[:, (n - 1) * P * PACK : n * P * PACK])
+            tower(w2_mx, x_dst, n, d_rest[:, (n - 1) * TILE_VALUES : n * TILE_VALUES])
         w1_mx = quantize([w1_bf[:]], "w1")
-        head_dst = keep.tile([P, V], F32, name="head_dst", tag="w1_bf", align_bytes=64)
+        head_dst = keep.tile([P, V], F32, name="head_dst", tag="w1_bf", align_bytes=MX_ALIGN)
         nc.vector.tensor_copy(head_dst[:], head_sb[:].indirect(dst_list[:]))
-        d_mx = quantize([d_first[:], d_rest[:, : P * PACK], d_rest[:, P * PACK :]], "d")
-
-        minus_y, e, total = {}, {}, {}
+        d_mx = quantize([d_first[:], d_rest[:, :TILE_VALUES], d_rest[:, TILE_VALUES:]], "d")
 
         def dependents(n):
-            p_bf = keep.tile([P, P * PACK], BF16, name="p_bf%d" % n, align_bytes=64)
+            p_bf = keep.tile([P, TILE_VALUES], BF16, name="p_bf%d" % n, align_bytes=MX_ALIGN)
             tower(w1_mx, x_offs, n, p_bf[:])
             return quantize([p_bf[:]], "p%d" % n)
 
+        p_mx = [dependents(n) for n in range(TILES)]
+
+        head_bank = psum.tile([P, TILES, P], F32, name="bank")
+        for b in range(TILES):
+            nc.tensor.transpose(head_bank[:, b, :], head_dst[:, block(b)], identity[:])
+        minus_head = keep.tile([P, TILES], F32, name="minus_head")
+        nc.scalar.activation(minus_head[:], head_bank[:, :, 0], ACT.Copy, scale=-1.0)
+
+        minus_y, exps, totals = {}, {}, {}
+
         def scores_by_rows(n):
-            bank = psum.tile([P, PACK, P], F32, name="bank")
-            scores = bank[:].rearrange("p t n -> p (t n)")
-            nc.tensor.matmul_mx(
-                out=scores,
-                lhsT=p_mx[n][0][:].bitcast(FP8X4),
-                lhsT_scale=p_mx[n][1][:],
-                rhs=d_mx[0][:].bitcast(FP8X4),
-                rhs_scale=d_mx[1][:],
-                start=True,
-                stop=True,
-            )
+            bank = psum.tile([P, TILES, P], F32, name="bank")
+            scores = bank[:].rearrange("p b j -> p (b j)")
+            multiply(scores, p_mx[n], block(0), d_mx, slice(0, V))
             summed = keep.tile([P, V], F32, name="minus_y%d" % n)
             nc.vector.scalar_tensor_tensor(summed[:], scores, -1.0, head_dst[:], ALU.mult, ALU.subtract)
             minus_y[n] = summed[:]
 
         def scores_by_columns(n):
-            bank = psum.tile([P, PACK, P], F32, name="bank")
+            bank = psum.tile([P, TILES, P], F32, name="bank")
             turned = keep.tile([P, TILES, P], F32, name="turned%d" % n)
             for b in range(TILES):
-                cols = slice(b * P, (b + 1) * P)
-                nc.tensor.matmul_mx(
-                    out=bank[:, b, :],
-                    lhsT=d_mx[0][:, cols].bitcast(FP8X4),
-                    lhsT_scale=d_mx[1][:, cols],
-                    rhs=p_mx[n][0][:].bitcast(FP8X4),
-                    rhs_scale=p_mx[n][1][:],
-                    start=True,
-                    stop=True,
-                )
+                multiply(bank[:, b, :], d_mx, block(b), p_mx[n], block(0))
             for b in range(TILES):
                 nc.scalar.activation(turned[:, b, :], bank[:, b, :], ACT.Identity, bias=minus_head[:, b : b + 1], scale=-1.0)
             return turned
 
         def turn_back(n, turned):
-            bank = psum.tile([P, PACK, P], F32, name="bank")
+            bank = psum.tile([P, TILES, P], F32, name="bank")
             for b in range(TILES):
                 nc.tensor.transpose(bank[:, b, :], turned[:, b, :], identity[:])
-            minus_y[n] = bank[:].rearrange("p t n -> p (t n)")
+            minus_y[n] = bank[:].rearrange("p b j -> p (b j)")
 
-        def exponentiate(n):
-            minus_max = keep.tile([P, 1], F32, name="minus_max%d" % n, tag="total0" if n == 3 else "minus_max%d" % n)
+        def exponentiate(n, tag):
+            minus_max = keep.tile([P, 1], F32, name="minus_max%d" % n, tag=tag)
             nc.vector.tensor_reduce(minus_max[:], minus_y[n], AX.X, ALU.min)
-            e[n] = keep.tile([P, V], F32, name="e%d" % n)
-            total[n] = keep.tile([P, 1], F32, name="total%d" % n)
-            nc.scalar.activation(e[n][:], minus_y[n], ACT.Exp, bias=minus_max[:], scale=-1.0, accum_out=total[n][:])
+            exps[n] = keep.tile([P, V], F32, name="exps%d" % n)
+            totals[n] = keep.tile([P, 1], F32, name="total%d" % n)
+            nc.scalar.activation(exps[n][:], minus_y[n], ACT.Exp, bias=minus_max[:], scale=-1.0, accum_out=totals[n][:])
 
-        def normalise(n, last=False):
+        def inverse_and_result(n):
             inverse = keep.tile([P, 1], F32, name="inverse%d" % n)
-            nc.vector.reciprocal(inverse[:], total[n][:])
-            result = keep.tile([P, V], F32, name="result%d" % n)
-            if last:
-                for u, queue in enumerate((nc.sync, nc.scalar)):
-                    cols = slice(u * V // 2, (u + 1) * V // 2)
-                    nc.vector.tensor_scalar(result[:, cols], e[n][:, cols], inverse[:], None, ALU.mult)
-                    queue.dma_start(out[n * P : (n + 1) * P, cols], result[:, cols])
-            else:
-                if n > 0:
-                    nc.vector.tensor_scalar(result[:], e[n][:], inverse[:], None, ALU.mult)
-                else:
-                    nc.gpsimd.tensor_scalar(result[:], e[n][:], inverse[:], 0.0, ALU.mult, ALU.add)
-                nc.sync.dma_start(out[n * P : (n + 1) * P, :], result[:])
-
-        p_mx = [dependents(n) for n in range(TILES)]
-
-        head_bank = psum.tile([P, PACK, P], F32, name="bank")
-        for b in range(TILES):
-            nc.tensor.transpose(head_bank[:, b, :], head_dst[:, b * P : (b + 1) * P], identity[:])
-        minus_head = keep.tile([P, TILES], F32, name="minus_head")
-        nc.scalar.activation(minus_head[:], head_bank[:, :, 0], ACT.Copy, scale=-1.0)
+            nc.vector.reciprocal(inverse[:], totals[n][:])
+            return inverse, keep.tile([P, V], F32, name="result%d" % n)
 
         scores_by_rows(0)
         turned1 = scores_by_columns(1)
         scores_by_rows(2)
         turned3 = scores_by_columns(3)
-        exponentiate(0)
+        exponentiate(0, "minus_max0")
         turn_back(1, turned1)
-        exponentiate(2)
+        exponentiate(2, "minus_max2")
         turn_back(3, turned3)
-        exponentiate(1)
-        normalise(0)
-        exponentiate(3)
-        normalise(2)
-        normalise(1)
-        normalise(3, last=True)
+        exponentiate(1, "minus_max1")
+
+        inverse, result = inverse_and_result(0)
+        nc.gpsimd.tensor_scalar(result[:], exps[0][:], inverse[:], 0.0, ALU.mult, ALU.add)
+        nc.sync.dma_start(out[block(0), :], result[:])
+
+        exponentiate(3, "total0")
+        for n in (2, 1):
+            inverse, result = inverse_and_result(n)
+            nc.vector.tensor_scalar(result[:], exps[n][:], inverse[:], None, ALU.mult)
+            nc.sync.dma_start(out[block(n), :], result[:])
+
+        inverse, result = inverse_and_result(3)
+        left, right = slice(0, LAST_VECTOR_COLUMNS), slice(LAST_VECTOR_COLUMNS, V)
+        nc.vector.tensor_scalar(result[:, left], exps[3][:, left], inverse[:], None, ALU.mult)
+        nc.sync.dma_start(out[block(3), left], result[:, left])
+        nc.scalar.activation(result[:, right], exps[3][:, right], ACT.Copy, scale=inverse[:])
+        nc.scalar.dma_start(out[block(3), right], result[:, right])

from contextlib import ExitStack

import concourse.mybir as mybir
from concourse.masks import make_identity

K, T, S, V, H = 512, 1024, 512, 512, 512
FLOPS = 2 * K * H * S + 2 * K * H * V + 2 * H * S * V

F32 = mybir.dt.float32
BF16 = mybir.dt.bfloat16
U32 = mybir.dt.uint32
I32 = mybir.dt.int32
U16 = mybir.dt.uint16
U8 = mybir.dt.uint8
FP8X4 = mybir.dt.float8_e4m3fn_x4
ALU = mybir.AluOpType
ACT = mybir.ActivationFunctionType
AX = mybir.AxisListType

P = 128
PACK = 4
TILES = 4
BANKS = 8
QUADRANT = 32
LIST_ROWS = 16
RUN = 4
HALF_GROUPS = H // 2 // (PACK * RUN)
TILE_VALUES = P * PACK
MX_ALIGN = 64
LAST_VECTOR_COLUMNS = 320


def tile_picked_zarc_relu_p_kernel(tc, x_words, x_scales, w1, w2, head, offs, dst, out):
    nc = tc.nc
    with ExitStack() as ctx:
        keep = ctx.enter_context(tc.tile_pool(name="keep", bufs=1))
        psum = ctx.enter_context(tc.psum_pool(name="psum", bufs=BANKS))

        dst_list = keep.tile([P, V // LIST_ROWS], U16, name="dst_list")
        offs_list = keep.tile([P, S // LIST_ROWS], U16, name="offs_list")
        words = keep.tile([P, T], I32, name="words", align_bytes=MX_ALIGN)
        scales = keep.tile([P, T], U8, name="scales", align_bytes=MX_ALIGN)
        head_sb = keep.tile([P, T], F32, name="head_sb")

        identity = keep.tile([P, P], F32, name="identity")
        make_identity(nc, identity[:])

        def load_weight_half(w, name, half):
            raw = keep.tile([P, PACK, H // 2], F32, name="%s_raw%d" % (name, half), align_bytes=MX_ALIGN)
            cols = slice(half * H // 2, (half + 1) * H // 2)
            nc.sync.dma_start(raw[:], w.rearrange("(p j) c -> p j c", j=PACK)[:, :, cols])
            return raw

        nc.sync.dma_start(dst_list[:], dst)
        scale_rows = x_scales[0].bitcast(I32)
        for q in range(P // QUADRANT):
            queue = nc.scalar if q % 2 else nc.sync
            queue.dma_start(
                scales[QUADRANT * q : QUADRANT * (q + 1), :].bitcast(I32),
                scale_rows[4 * q : 4 * q + 4, :].unsqueeze(0).to_broadcast([QUADRANT // 4, 4, T // 4]),
            )
        nc.sync.dma_start(offs_list[:], offs)
        w2_raw = [load_weight_half(w2, "w2", half) for half in range(2)]
        nc.sync.dma_start(words[:], x_words[0].rearrange("p c r -> p (c r)").bitcast(I32))
        w1_raw = [load_weight_half(w1, "w1", half) for half in range(2)]
        nc.sync.dma_start(head_sb[:], head)

        def gather_scales(index_list, name):
            picked = keep.tile([P, S], U8, name=name + "_scales", align_bytes=MX_ALIGN)
            nc.vector.tensor_copy(picked[:], scales[:].indirect(index_list[:]))
            return picked

        def gather_words(index_list, name, pieces, tag):
            picked = keep.tile([P, S], U32, name=name + "_codes", tag=tag, align_bytes=MX_ALIGN)
            width = S // pieces
            for u in range(pieces):
                entries = index_list[:, u * width // LIST_ROWS : (u + 1) * width // LIST_ROWS]
                nc.vector.tensor_copy(picked[:, u * width : (u + 1) * width], words[:].bitcast(U32).indirect(entries))
            return picked

        def round_weight(copy, woven, raw, half, first_slot, slots):
            groups = slice(HALF_GROUPS * half, HALF_GROUPS * (half + 1))
            copy(
                woven.rearrange("p (t a r j) -> p a t j r", t=slots, r=RUN, j=PACK)[:, groups],
                raw[:].rearrange("p j (a t r) -> p a t j r", t=PACK, r=RUN)[:, :, first_slot : first_slot + slots],
            )

        def quantize(pieces, name):
            width = sum(piece.shape[1] for piece in pieces) // PACK
            codes = keep.tile([P, width], U32, name=name + "_codes", align_bytes=MX_ALIGN)
            scale_bytes = keep.tile([P, width], U8, name=name + "_scales", align_bytes=MX_ALIGN)
            first = 0
            for piece in pieces:
                cols = slice(first, first + piece.shape[1] // PACK)
                nc.vector.quantize_mx(out=codes[:, cols].bitcast(FP8X4), scales=scale_bytes[:, cols], in_=piece)
                first = cols.stop
            return codes, scale_bytes

        def multiply(result, stationary, stationary_cols, moving, moving_cols):
            nc.tensor.matmul_mx(
                out=result,
                lhsT=stationary[0][:, stationary_cols].bitcast(FP8X4),
                lhsT_scale=stationary[1][:, stationary_cols],
                rhs=moving[0][:, moving_cols].bitcast(FP8X4),
                rhs_scale=moving[1][:, moving_cols],
                start=True,
                stop=True,
            )

        def block(n):
            return slice(n * P, (n + 1) * P)

        def tower(weight, picked, n, hidden, on_vector=False):
            bank = psum.tile([P, PACK, P], F32, name="bank")
            for t in range(PACK):
                multiply(bank[:, t, :], weight, block(t), picked, block(n))
            woven = hidden.rearrange("p (n t) -> p n t", t=PACK)
            sums = bank[:].rearrange("p t n -> p n t")
            if on_vector:
                nc.vector.tensor_scalar(woven, sums, 0.0, None, ALU.max)
            else:
                nc.scalar.activation(woven, sums, ACT.Relu)

        dst_scales = gather_scales(dst_list, "x_dst")
        offs_scales = gather_scales(offs_list, "x_offs")

        w2_low = keep.tile([P, 2 * TILE_VALUES], BF16, name="w2_low", align_bytes=MX_ALIGN)
        w2_high = keep.tile([P, 2 * TILE_VALUES], BF16, name="w2_high", align_bytes=MX_ALIGN)
        round_weight(nc.scalar.copy, w2_low[:], w2_raw[0], 0, 0, 2)
        round_weight(nc.scalar.copy, w2_high[:], w2_raw[0], 0, 2, 2)
        round_weight(nc.scalar.copy, w2_low[:], w2_raw[1], 1, 0, 2)
        round_weight(nc.vector.tensor_copy, w2_high[:], w2_raw[1], 1, 2, 2)
        w2_mx = quantize([w2_low[:], w2_high[:]], "w2")
        x_dst = (gather_words(dst_list, "x_dst", 2, "w2_high"), dst_scales)
        x_offs = (gather_words(offs_list, "x_offs", 1, "w2_low"), offs_scales)

        w1_bf = keep.tile([P, H * PACK], BF16, name="w1_bf", align_bytes=MX_ALIGN)
        for half in range(2):
            round_weight(nc.scalar.copy, w1_bf[:], w1_raw[half], half, 0, PACK)

        d_first = keep.tile([P, TILE_VALUES], BF16, name="d_first", align_bytes=MX_ALIGN)
        d_rest = keep.tile([P, (TILES - 1) * TILE_VALUES], BF16, name="d_rest", tag="w1_raw1", align_bytes=MX_ALIGN)
        tower(w2_mx, x_dst, 0, d_first[:], on_vector=True)
        for n in range(1, TILES):
            tower(w2_mx, x_dst, n, d_rest[:, (n - 1) * TILE_VALUES : n * TILE_VALUES])
        w1_mx = quantize([w1_bf[:]], "w1")
        head_dst = keep.tile([P, V], F32, name="head_dst", tag="w1_bf", align_bytes=MX_ALIGN)
        nc.vector.tensor_copy(head_dst[:], head_sb[:].indirect(dst_list[:]))
        d_mx = quantize([d_first[:], d_rest[:, :TILE_VALUES], d_rest[:, TILE_VALUES:]], "d")

        def dependents(n):
            p_bf = keep.tile([P, TILE_VALUES], BF16, name="p_bf%d" % n, align_bytes=MX_ALIGN)
            tower(w1_mx, x_offs, n, p_bf[:])
            return quantize([p_bf[:]], "p%d" % n)

        p_mx = [dependents(n) for n in range(TILES)]

        head_bank = psum.tile([P, TILES, P], F32, name="bank")
        for b in range(TILES):
            nc.tensor.transpose(head_bank[:, b, :], head_dst[:, block(b)], identity[:])
        minus_head = keep.tile([P, TILES], F32, name="minus_head")
        nc.scalar.activation(minus_head[:], head_bank[:, :, 0], ACT.Copy, scale=-1.0)

        minus_y, exps, totals = {}, {}, {}

        def scores_by_rows(n):
            bank = psum.tile([P, TILES, P], F32, name="bank")
            scores = bank[:].rearrange("p b j -> p (b j)")
            multiply(scores, p_mx[n], block(0), d_mx, slice(0, V))
            summed = keep.tile([P, V], F32, name="minus_y%d" % n)
            nc.vector.scalar_tensor_tensor(summed[:], scores, -1.0, head_dst[:], ALU.mult, ALU.subtract)
            minus_y[n] = summed[:]

        def scores_by_columns(n):
            bank = psum.tile([P, TILES, P], F32, name="bank")
            turned = keep.tile([P, TILES, P], F32, name="turned%d" % n)
            for b in range(TILES):
                multiply(bank[:, b, :], d_mx, block(b), p_mx[n], block(0))
            for b in range(TILES):
                nc.scalar.activation(turned[:, b, :], bank[:, b, :], ACT.Identity, bias=minus_head[:, b : b + 1], scale=-1.0)
            return turned

        def turn_back(n, turned):
            bank = psum.tile([P, TILES, P], F32, name="bank")
            for b in range(TILES):
                nc.tensor.transpose(bank[:, b, :], turned[:, b, :], identity[:])
            minus_y[n] = bank[:].rearrange("p b j -> p (b j)")

        def exponentiate(n, tag):
            minus_max = keep.tile([P, 1], F32, name="minus_max%d" % n, tag=tag)
            nc.vector.tensor_reduce(minus_max[:], minus_y[n], AX.X, ALU.min)
            exps[n] = keep.tile([P, V], F32, name="exps%d" % n)
            totals[n] = keep.tile([P, 1], F32, name="total%d" % n)
            nc.scalar.activation(exps[n][:], minus_y[n], ACT.Exp, bias=minus_max[:], scale=-1.0, accum_out=totals[n][:])

        def inverse_and_result(n):
            inverse = keep.tile([P, 1], F32, name="inverse%d" % n)
            nc.vector.reciprocal(inverse[:], totals[n][:])
            return inverse, keep.tile([P, V], F32, name="result%d" % n)

        scores_by_rows(0)
        turned1 = scores_by_columns(1)
        scores_by_rows(2)
        turned3 = scores_by_columns(3)
        exponentiate(0, "minus_max0")
        turn_back(1, turned1)
        exponentiate(2, "minus_max2")
        turn_back(3, turned3)
        exponentiate(1, "minus_max1")

        inverse, result = inverse_and_result(0)
        nc.gpsimd.tensor_scalar(result[:], exps[0][:], inverse[:], 0.0, ALU.mult, ALU.add)
        nc.sync.dma_start(out[block(0), :], result[:])

        exponentiate(3, "total0")
        for n in (2, 1):
            inverse, result = inverse_and_result(n)
            nc.vector.tensor_scalar(result[:], exps[n][:], inverse[:], None, ALU.mult)
            nc.sync.dma_start(out[block(n), :], result[:])

        inverse, result = inverse_and_result(3)
        left, right = slice(0, LAST_VECTOR_COLUMNS), slice(LAST_VECTOR_COLUMNS, V)
        nc.vector.tensor_scalar(result[:, left], exps[3][:, left], inverse[:], None, ALU.mult)
        nc.sync.dma_start(out[block(3), left], result[:, left])
        nc.scalar.activation(result[:, right], exps[3][:, right], ACT.Copy, scale=inverse[:])
        nc.scalar.dma_start(out[block(3), right], result[:, right])
